import numpy as np
import ml_dtypes


def mxq(x, axis, fmt="e4m3"):
    dtype, down = {"e4m3": (ml_dtypes.float8_e4m3fn, 7), "e5m2": (ml_dtypes.float8_e5m2, 14)}[fmt]
    v = np.moveaxis(np.asarray(x, np.float32).astype(ml_dtypes.bfloat16).astype(np.float64), axis, -1)
    blocks = v.reshape(v.shape[:-1] + (-1, 32))
    amax = np.abs(blocks).max(-1, keepdims=True)
    byte = np.maximum(np.where(amax > 0, np.frexp(amax)[1] - 1 + 127, 0) - down, 1)
    scale = np.exp2(byte - 127.0)
    codes = (blocks / scale).astype(np.float32).astype(dtype).astype(np.float64)
    return np.moveaxis((codes * scale).reshape(v.shape), -1, axis)


WIDE = False


def mx_kscale(k):
    if not WIDE:
        return np.ones(k)
    levels = np.array([10, -10, 5, -5, 0])
    if k % 512:
        return np.exp2(np.random.permutation(np.resize(levels, k // 32))).repeat(32)
    a = np.empty((k // 512, 16))
    for p in range(k // 512):
        a[p, :8] = np.random.permutation(np.resize(levels, 8))
        for g in range(8):
            far = levels[np.abs(levels - a[p, g]) >= 10]
            a[p, g + 8] = far[np.random.randint(len(far))]
    return np.exp2(a.ravel()).repeat(32)


def f64(x):
    return np.asarray(x).astype(np.float64)


def striped(idx):
    return np.tile(idx.reshape(-1, 16).T, (8, 1)).astype(np.uint16)


def unstriped(offs):
    return offs[:16].T.reshape(-1).astype(np.int64)


E2M1 = np.array([0.0, 0.5, 1.0, 1.5, 2.0, 3.0, 4.0, 6.0, -0.0, -0.5, -1.0, -1.5, -2.0, -3.0, -4.0, -6.0])


def pack_weight(w, fmt):
    k, n = w.shape
    w = f64(np.asarray(w, np.float32).astype(ml_dtypes.bfloat16)).reshape(k // 32, 32, n)
    amax = np.abs(w).max(1)
    if fmt == "e4m3":
        byte = np.frexp(amax)[1] - 1 + 127 - 7
    else:
        mant, ex = np.frexp(amax / 6.0)
        byte = np.where(mant > 0.5, ex, ex - 1) + 127
    byte = np.clip(np.where(amax > 0, byte, 1), 1, 254)
    scaled = (w * np.exp2(127.0 - byte)[:, None, :]).reshape(k, n).astype(np.float32)
    by_word = np.ascontiguousarray(scaled.reshape(k // 512, 128, 4, n).transpose(0, 1, 3, 2))
    if fmt == "e4m3":
        words = by_word.astype(ml_dtypes.float8_e4m3fn).view(np.uint8)
    else:
        c = by_word.astype(ml_dtypes.float4_e2m1fn).view(np.uint8) & 0xF
        words = (c[..., 0::2] | (c[..., 1::2] << 4)).reshape(k // 512, 128, 2 * n)
    return np.ascontiguousarray(words), np.ascontiguousarray(byte.astype(np.uint8).reshape(k // 512, 16, n))


def unpack_weight(words, scales, fmt):
    g, _, n = scales.shape
    words = np.ascontiguousarray(words).reshape(g, 128, n, -1)
    if fmt == "e4m3":
        vals = words.view(ml_dtypes.float8_e4m3fn).astype(np.float64)
    else:
        nib = np.empty((g, 128, n, 4), np.uint8)
        nib[..., 0::2] = words & 0xF
        nib[..., 1::2] = words >> 4
        vals = E2M1[nib]
    vals = vals * np.repeat(np.exp2(scales.astype(np.float64) - 127.0), 8, axis=1)[..., None]
    return vals.transpose(0, 1, 3, 2).reshape(g * 512, n)


def gelu(v):
    return 0.5 * v * (1.0 + np.tanh(np.sqrt(2.0 / np.pi) * (v + 0.044715 * v**3)))


def bf(x):
    return np.asarray(x, np.float32).astype(ml_dtypes.bfloat16)


def planes(Y):
    n, m = Y.shape
    b = f64(bf(Y)).reshape(n // 32, 32, m)
    amax = np.abs(b).max(1)
    byte = np.clip(np.where(amax > 0, np.frexp(amax)[1] - 1 + 127 - 7, 1), 1, 254)
    codes = (b * np.exp2(127.0 - byte)[:, None, :]).reshape(n, m).astype(np.float32).astype(ml_dtypes.float8_e4m3fn).view(np.uint8)
    words = codes.reshape(n // 512, 128, 4, m).transpose(0, 1, 3, 2)
    return np.ascontiguousarray(words), np.ascontiguousarray(byte.astype(np.uint8).reshape(n // 512, 16, m))


K, T, S, H, N = 1024, 2048, 512, 1024, 512

def setup_inputs():
    n = np.random.standard_normal
    s = mx_kscale(K)[:, None]
    u = mx_kscale(H)[:, None]
    tab_words, tab_scales = pack_weight(n((K, T)) * s, "e4m3")
    w2_words, w2_scales = pack_weight(0.5 * n((K, H)) / np.sqrt(K) / s * u.T, "e2m1")
    w4_words, w4_scales = pack_weight(n((H, N)) / np.sqrt(H) / u, "e4m3")
    return {
        "tab_words": tab_words, "tab_scales": tab_scales,
        "offs": striped(np.random.permutation(T)[:S]),
        "offs2": striped(np.random.permutation(T)[:S]),
        "offs3": striped(np.random.permutation(T)[:S]),
        "w1": (0.55 * n((K, H)) / np.sqrt(K) / s).astype(np.float32),
        "w2_words": w2_words, "w2_scales": w2_scales,
        "w3": (0.9 * n((K, H)) / np.sqrt(K) / s * u.T).astype(np.float32),
        "amp": (1.5 * np.exp(0.2 * n(H)) * u[:, 0]).astype(np.float32),
        "w4_words": w4_words, "w4_scales": w4_scales,
        "gain": np.exp(0.8 * n(N)).astype(np.float32),
    }

def reference(tab_words, tab_scales, offs, offs2, offs3, w1, w2_words, w2_scales, w3, amp, w4_words, w4_scales, gain):
    TW = unpack_weight(tab_words, tab_scales, "e4m3")
    v = TW[:, unstriped(offs)]
    v2 = TW[:, unstriped(offs2)]
    v3 = TW[:, unstriped(offs3)]
    w2 = unpack_weight(w2_words, w2_scales, "e2m1")
    w4 = unpack_weight(w4_words, w4_scales, "e4m3")
    prefix = mxq(f64(w1), 0, "e4m3").T @ v
    carrier = w2.T @ v2
    site = mxq(f64(w3), 0, "e4m3").T @ v3
    path = f64(amp)[:, None] * np.sin(prefix) + carrier
    h = np.maximum(path, site)
    y = f64(gain)[:, None] * (w4.T @ mxq(h, 0, "e4m3"))
    words, scales = planes(y)
    return y, words, scales

@@ -1,0 +1,360 @@
+import math
+from contextlib import ExitStack
+
+import concourse.mybir as mybir
+
+K, T, S, H, N = 1024, 2048, 512, 1024, 512
+FLOPS = 2 * (3 * K * H * S + H * N * S)
+
+F32 = mybir.dt.float32
+BF16 = mybir.dt.bfloat16
+I32 = mybir.dt.int32
+U32 = mybir.dt.uint32
+U16 = mybir.dt.uint16
+U8 = mybir.dt.uint8
+FP8X4 = mybir.dt.float8_e4m3fn_x4
+FP4X4 = mybir.dt.float4_e2m1fn_x4
+ACT = mybir.ActivationFunctionType
+ALU = mybir.AluOpType
+
+P = 128
+PACK = 4
+GROUP = P * PACK
+PASSES = K // GROUP
+GROUPS = H // GROUP
+QUADS = 4
+HALF = S // 2
+RAW_BUFS = 4
+
+
+def tile_list_anycast_steering_features_kernel(
+    tc, tab_words, tab_scales, offs, offs2, offs3, w1, w2_words, w2_scales, w3, amp,
+    w4_words, w4_scales, gain, out_0, out_1, out_2,
+):
+    nc = tc.nc
+
+    def copy_on(engine, out, in_):
+        if engine == "scalar":
+            nc.scalar.copy(out=out, in_=in_)
+        elif engine == "gpsimd":
+            nc.gpsimd.tensor_scalar(out=out, in0=in_, scalar1=1.0, scalar2=0.0, op0=ALU.mult, op1=ALU.add)
+        else:
+            nc.vector.tensor_copy(out=out, in_=in_)
+
+    with ExitStack() as ctx:
+        keep = ctx.enter_context(tc.tile_pool(name="keep", bufs=1))
+        stream = ctx.enter_context(tc.tile_pool(name="stream", bufs=1))
+        ring = ctx.enter_context(tc.tile_pool(name="ring", bufs=3))
+        psum = ctx.enter_context(tc.psum_pool(name="psum", bufs=8))
+
+        def kept(shape, dtype, name):
+            return keep.tile(shape, dtype, name=name, align_bytes=64)
+
+        lists = [keep.tile([P, S // 16], U16, name="list%d" % i) for i in range(3)]
+        table = [kept([P, T], U32, "table%d" % a) for a in range(PASSES)]
+        table_scales = kept([P, T], U8, "table_scales")
+        weight_scales_raw = kept([P, PASSES * H], U8, "weight_scales_raw")
+        weight_scales = kept([P, PASSES * H], U8, "weight_scales")
+        table_rows = kept([P, T // 4], I32, "table_rows")
+        w2_rows = kept([P, PASSES * H // 4], I32, "w2_rows")
+        carrier_plane1 = kept([P, S], U8, "carrier_plane1")
+        w2_raw = keep.tile([P, PASSES * 2 * H], U8, name="w2_raw", tag="packed_raw", align_bytes=64)
+        w2_codes = kept([P, PASSES * 2 * H], U8, "w2_codes")
+        amp_sb = kept([P, GROUPS, PACK], F32, "amp_sb")
+        w4_rows = kept([P, N // 4], I32, "w4_rows")
+        gain_sb = kept([P, PACK], F32, "gain_sb")
+        one = kept([P, 1], F32, "one")
+        quarter_pi = kept([P, 1], F32, "quarter_pi")
+
+        nc.gpsimd.memset(weight_scales_raw[:].bitcast(I32), 0)
+        nc.vector.memset(table_scales[:].bitcast(I32), 0)
+        nc.gpsimd.memset(carrier_plane1[:].bitcast(I32), 0)
+        nc.vector.memset(one[:], 1.0)
+        nc.vector.tensor_scalar(out=quarter_pi[:], in0=one[:], scalar1=math.pi / 4, scalar2=None, op0=ALU.mult)
+
+        raw = {}
+
+        def load_weight(name, w, b, a, parts):
+            rows = w[a * GROUP : (a + 1) * GROUP, :].rearrange("(p j) c -> p j c", j=PACK)
+            width = GROUP // parts
+            raw[name, b, a] = []
+            for u in range(parts):
+                piece = stream.tile([P, PACK, width], F32, name="piece", bufs=RAW_BUFS)
+                c0 = b * GROUP + u * width
+                nc.sync.dma_start(out=piece[:], in_=rows[:, :, c0 : c0 + width])
+                raw[name, b, a].append(piece)
+
+        def load_table(a):
+            nc.sync.dma_start(
+                out=table[a][:].bitcast(I32), in_=tab_words[a].rearrange("p n i -> p (n i)").bitcast(I32)
+            )
+
+        for q in range(QUADS):
+            nc.sync.dma_start(
+                out=table_rows[32 * q : 32 * q + 8, :], in_=tab_scales[:, 4 * q : 4 * q + 4, :].bitcast(I32)
+            )
+        nc.sync.dma_start(lists[1][:], offs2)
+        nc.sync.dma_start(lists[0][:], offs)
+        nc.sync.dma_start(
+            out=w2_raw[:].bitcast(I32).rearrange("p (a c) -> p a c", a=PASSES),
+            in_=w2_words.bitcast(I32).rearrange("a p c -> p a c"),
+        )
+        load_table(0)
+        nc.sync.dma_start(lists[2][:], offs3)
+        for q in range(QUADS):
+            nc.sync.dma_start(
+                out=w2_rows[32 * q : 32 * q + 4, :].rearrange("r (a c) -> r a c", a=PASSES),
+                in_=w2_scales[:, 4 * q : 4 * q + 4, :].bitcast(I32).rearrange("a r c -> r a c"),
+            )
+        load_weight("w1", w1, 0, 0, 1)
+        load_weight("w1", w1, 0, 1, 1)
+        load_table(1)
+        load_weight("w1", w1, 1, 0, 1)
+        nc.sync.dma_start(out=amp_sb[:], in_=amp.rearrange("(b p t) -> p b t", p=P, t=PACK))
+        nc.sync.dma_start(out=gain_sb[:], in_=gain.rearrange("(p t) -> p t", t=PACK))
+        load_weight("w1", w1, 1, 1, 1)
+        for q in range(QUADS):
+            nc.sync.dma_start(
+                out=w4_rows[32 * q : 32 * q + 8, :], in_=w4_scales[:, 4 * q : 4 * q + 4, :].bitcast(I32)
+            )
+
+
+        for q in range(QUADS):
+            rows = slice(32 * q, 32 * q + 8)
+            nc.vector.tensor_copy(out=table_scales[rows, :].bitcast(I32), in_=table_rows[rows, :])
+        nc.scalar.copy(
+            out=w2_codes[:].bitcast(U16).rearrange("p (g t m) -> p g t m", t=PACK, m=P),
+            in_=w2_raw[:].bitcast(U16).rearrange("p (g m t) -> p g t m", t=PACK, m=P),
+        )
+        for q in range(QUADS):
+            rows = slice(32 * q, 32 * q + 4)
+            nc.scalar.copy(out=weight_scales_raw[rows, :].bitcast(U32), in_=w2_rows[rows, :].bitcast(U32))
+        w4_raw = keep.tile([P, GROUPS * N], I32, name="w4_raw", tag="packed_raw", align_bytes=64)
+        nc.sync.dma_start(
+            out=w4_raw[:].rearrange("p (a c) -> p a c", a=GROUPS),
+            in_=w4_words.rearrange("a p c i -> p a (c i)").bitcast(I32),
+        )
+
+        picked = {}
+        picked_scales = {}
+
+        def gather_words(i, a, tag=None):
+            name = "picked%d_%d" % (i, a)
+            picked[i, a] = keep.tile([P, S], U32, name=name, tag=tag or name, align_bytes=64)
+            nc.vector.tensor_copy(out=picked[i, a][:], in_=table[a][:].indirect(lists[i][:]))
+
+        def gather_scales(i):
+            picked_scales[i] = kept([P, S], U8, "picked_scales%d" % i)
+            nc.vector.tensor_copy(out=picked_scales[i][:], in_=table_scales[:].indirect(lists[i][:]))
+
+        grouped = {}
+        codes = {}
+        planes = {}
+
+        def round_weight(name, b, a, engines):
+            tile = kept([P, GROUP * PACK], BF16, "grouped_%s_%d_%d" % (name, b, a))
+            grouped[name, b, a] = tile
+            dst = tile[:].rearrange("p (t m j) -> p m j t", t=PACK, j=PACK)
+            pieces = raw[name, b, a]
+            share = P // len(engines)
+            per_piece = P // len(pieces)
+            for u, engine in enumerate(engines):
+                m0 = u * share
+                src = pieces[m0 // per_piece][:].rearrange("p j (m t) -> p m j t", t=PACK)
+                l0 = m0 % per_piece
+                copy_on(engine, dst[:, m0 : m0 + share], src[:, l0 : l0 + share])
+
+        def quantize_weight(name, b, a):
+            codes[name, b, a] = kept([P, GROUP], U32, "codes_%s_%d_%d" % (name, b, a))
+            planes[name, b, a] = kept([P, GROUP], U8, "plane_%s_%d_%d" % (name, b, a))
+            nc.vector.quantize_mx(
+                out=codes[name, b, a][:].bitcast(FP8X4), scales=planes[name, b, a][:], in_=grouped[name, b, a][:]
+            )
+
+        def product(name, i, b):
+            banks = [psum.tile([P, S], F32, name="bank", tag="bank") for t in range(PACK)]
+            for a in range(PASSES):
+                for t in range(PACK):
+                    cols = slice(t * P, (t + 1) * P)
+                    nc.tensor.matmul_mx(
+                        out=banks[t][:],
+                        lhsT=codes[name, b, a][:, cols].bitcast(FP8X4),
+                        lhsT_scale=planes[name, b, a][:, cols],
+                        rhs=picked[i, a][:].bitcast(FP8X4),
+                        rhs_scale=picked_scales[i][4 * a : P, :],
+                        start=(a == 0),
+                        stop=(a == PASSES - 1),
+                    )
+            return banks
+
+        def carrier_product(b):
+            banks = [psum.tile([P, S], F32, name="bank", tag="bank") for t in range(PACK)]
+            for a in range(PASSES):
+                for t in range(PACK):
+                    c0 = a * H + b * GROUP + t * P
+                    nc.tensor.matmul_mx(
+                        out=banks[t][:],
+                        lhsT=w2_codes[:, 2 * c0 : 2 * (c0 + P)].bitcast(FP4X4),
+                        lhsT_scale=weight_scales[:, c0 : c0 + P],
+                        rhs=picked[1, a][:].bitcast(FP8X4),
+                        rhs_scale=(picked_scales[1] if a == 0 else carrier_plane1)[:],
+                        start=(a == 0),
+                        stop=(a == PASSES - 1),
+                    )
+            return banks
+
+        lifted = {}
+
+        def lifted_path(b, prefix, carrier):
+            for t in range(PACK):
+                sine = ring.tile([P, S], F32, name="sine")
+                square = ring.tile([P, S], F32, name="square")
+                nc.scalar.activation(out=sine[:], in_=prefix[t][:], func=ACT.Sin, bias=quarter_pi[:], scale=0.5)
+                nc.scalar.activation(out=square[:], in_=sine[:], func=ACT.Square, scale=math.sqrt(2.0))
+                lifted[b, t] = kept([P, S], F32, "lifted%d_%d" % (b, t))
+                nc.vector.scalar_tensor_tensor(
+                    out=lifted[b, t][:], in0=square[:], scalar=amp_sb[:, b, t : t + 1], in1=carrier[t][:],
+                    op0=ALU.mult, op1=ALU.add,
+                )
+
+        def interleave(engine, dst, src):
+            copy_on(
+                engine,
+                dst.rearrange("p (c i t) -> p c t i", i=PACK, t=PACK),
+                src.rearrange("p t (c i) -> p c t i", i=PACK),
+            )
+
+        h_codes = {}
+        h_planes = {}
+
+        def make_h(b, u, site, engine, width=HALF):
+            cols = slice(u * width, (u + 1) * width)
+            rows = kept([P, PACK, width], BF16, "h_rows%d_%d" % (b, u))
+            for t in range(PACK):
+                nc.vector.scalar_tensor_tensor(
+                    out=rows[:, t, :], in0=lifted[b, t][:, cols], scalar=amp_sb[:, b, t : t + 1], in1=site[t][:, cols],
+                    op0=ALU.subtract, op1=ALU.max,
+                )
+            woven = kept([P, PACK * width], BF16, "h_woven%d_%d" % (b, u))
+            interleave(engine, woven[:], rows[:])
+            return woven
+
+        def quantize_h(b, u, woven, width=HALF):
+            words = kept([P, width], U32, "h_codes%d_%d" % (b, u))
+            plane = kept([P, width], U8, "h_plane%d_%d" % (b, u))
+            nc.vector.quantize_mx(out=words[:].bitcast(FP8X4), scales=plane[:], in_=woven[:])
+            for v in range(width // HALF):
+                h_codes[b, u + v] = words[:, v * HALF : (v + 1) * HALF]
+                h_planes[b, u + v] = plane[:, v * HALF : (v + 1) * HALF]
+
+        def last_product(b, u, banks):
+            for t in range(PACK):
+                c0 = b * N + t * P
+                nc.tensor.matmul_mx(
+                    out=banks[u][t // 2][:, (t % 2) * HALF : (t % 2 + 1) * HALF],
+                    lhsT=w4_codes[:, c0 : c0 + P].bitcast(FP8X4),
+                    lhsT_scale=w4_planes[4 * b : P, t * P : (t + 1) * P],
+                    rhs=h_codes[b, u].bitcast(FP8X4),
+                    rhs_scale=h_planes[b, u],
+                    start=(b == 0 and t % 2 == 0),
+                    stop=(b == GROUPS - 1 and t % 2 == 1),
+                )
+
+        gather_scales(1)
+        nc.gpsimd.dma_start(
+            out=carrier_plane1[0 : P - 4, :].bitcast(I32), in_=picked_scales[1][4:P, :].bitcast(I32)
+        )
+        gather_scales(0)
+        gather_scales(2)
+        gather_words(0, 0)
+        gather_words(1, 0)
+        round_weight("w1", 0, 0, ["scalar"])
+        load_weight("w3", w3, 0, 0, 1)
+        gather_words(2, 0)
+        nc.vector.tensor_copy(
+            out=weight_scales[:].rearrange("p (g t m) -> p g t m", t=PACK, m=P),
+            in_=weight_scales_raw[:].rearrange("p (g m t) -> p g t m", t=PACK, m=P),
+        )
+        w4_scales_raw = keep.tile([P, N], U8, name="w4_scales_raw", tag="weight_scales_raw", align_bytes=64)
+        nc.gpsimd.memset(w4_scales_raw[:].bitcast(I32), 0)
+        for q in range(QUADS):
+            rows = slice(32 * q, 32 * q + 8)
+            nc.gpsimd.tensor_copy(out=w4_scales_raw[rows, :].bitcast(I32), in_=w4_rows[rows, :])
+        quantize_weight("w1", 0, 0)
+        round_weight("w1", 0, 1, ["scalar"])
+        load_weight("w3", w3, 0, 1, 1)
+        gather_words(0, 1, "grouped_w1_0_0")
+        quantize_weight("w1", 0, 1)
+        gather_words(1, 1, "grouped_w1_0_1")
+        prefix0 = product("w1", 0, 0)
+        carrier0 = carrier_product(0)
+        round_weight("w1", 1, 0, ["scalar"])
+        load_weight("w3", w3, 1, 0, 1)
+        gather_words(2, 1, "codes_w1_0_1")
+        quantize_weight("w1", 1, 0)
+        round_weight("w1", 1, 1, ["scalar"])
+        lifted_path(0, prefix0, carrier0)
+        quantize_weight("w1", 1, 1)
+        prefix1 = product("w1", 0, 1)
+        carrier1 = carrier_product(1)
+        round_weight("w3", 0, 0, ["vector"])
+        load_weight("w3", w3, 1, 1, 2)
+        w4_codes = keep.tile([P, GROUPS * N], I32, name="w4_codes", tag="codes_w1_1_0", align_bytes=64)
+        nc.vector.tensor_copy(
+            out=w4_codes[:].bitcast(I32).rearrange("p (g t m) -> p g m t", t=PACK, m=P),
+            in_=w4_raw[:].bitcast(I32).rearrange("p (g m t) -> p g m t", t=PACK, m=P),
+        )
+        w4_planes = keep.tile([P, N], U8, name="w4_planes", tag="plane_w1_1_0", align_bytes=64)
+        nc.vector.tensor_copy(
+            out=w4_planes[:].rearrange("p (t m) -> p t m", t=PACK),
+            in_=w4_scales_raw[:].rearrange("p (m t) -> p t m", t=PACK),
+        )
+        quantize_weight("w3", 0, 0)
+        round_weight("w3", 0, 1, ["vector"])
+        lifted_path(1, prefix1, carrier1)
+        quantize_weight("w3", 0, 1)
+        site0 = product("w3", 2, 0)
+        round_weight("w3", 1, 0, ["scalar"])
+        round_weight("w3", 1, 1, ["vector", "scalar"])
+        woven0 = make_h(0, 0, site0, "scalar", S)
+        quantize_weight("w3", 1, 0)
+        quantize_weight("w3", 1, 1)
+        site1 = product("w3", 2, 1)
+        quantize_h(0, 0, woven0, S)
+        y_banks = [[psum.tile([P, S], F32, name="bank", tag="bank") for pair in range(2)] for u in range(2)]
+        for u in range(2):
+            last_product(0, u, y_banks)
+
+        woven1 = [make_h(1, u, site1, ["scalar", "vector"][u]) for u in range(2)]
+        y_rows = out_0.rearrange("(p t) j -> p t j", t=PACK)
+        y_words = out_1[0].rearrange("p m i -> p (m i)").bitcast(I32)
+        y_plane = kept([P, S], U8, "y_plane")
+        y_woven = []
+        for u in range(2):
+            quantize_h(1, u, woven1[u])
+            last_product(1, u, y_banks)
+        for u in range(2):
+            cols = slice(u * HALF, (u + 1) * HALF)
+            y = kept([P, PACK, HALF], F32, "y%d" % u)
+            for t in range(PACK):
+                sums = y_banks[u][t // 2][:, (t % 2) * HALF : (t % 2 + 1) * HALF]
+                if t // 2 == 0:
+                    nc.scalar.activation(out=y[:, t, :], in_=sums, func=ACT.Copy, scale=gain_sb[:, t : t + 1])
+                else:
+                    nc.vector.tensor_scalar(
+                        out=y[:, t, :], in0=sums, scalar1=gain_sb[:, t : t + 1], scalar2=None, op0=ALU.mult
+                    )
+            nc.sync.dma_start(out=y_rows[:, :, cols], in_=y[:])
+            woven = kept([P, PACK * HALF], BF16, "y_woven%d" % u)
+            interleave(["vector", "vector"][u], woven[:], y[:])
+            y_woven.append(woven)
+        for u in range(2):
+            cols = slice(u * HALF, (u + 1) * HALF)
+            y_codes = kept([P, HALF], U32, "y_codes%d" % u)
+            nc.vector.quantize_mx(out=y_codes[:].bitcast(FP8X4), scales=y_plane[:, cols], in_=y_woven[u][:])
+            nc.sync.dma_start(out=y_words[:, cols], in_=y_codes[:].bitcast(I32))
+        for q in range(QUADS):
+            queue = nc.sync if q % 2 == 0 else nc.scalar
+            queue.dma_start(
+                out=out_2[0, 4 * q : 4 * q + 4, :].bitcast(I32), in_=y_plane[32 * q : 32 * q + 4, :].bitcast(I32)
+            )

@@ -44,7 +44,7 @@ def tile_list_anycast_steering_features_kernel(
     with ExitStack() as ctx:
         keep = ctx.enter_context(tc.tile_pool(name="keep", bufs=1))
         stream = ctx.enter_context(tc.tile_pool(name="stream", bufs=1))
-        ring = ctx.enter_context(tc.tile_pool(name="ring", bufs=3))
+        ring = ctx.enter_context(tc.tile_pool(name="ring", bufs=4))
         psum = ctx.enter_context(tc.psum_pool(name="psum", bufs=8))
 
         def kept(shape, dtype, name):
@@ -53,15 +53,14 @@ def tile_list_anycast_steering_features_kernel(
         lists = [keep.tile([P, S // 16], U16, name="list%d" % i) for i in range(3)]
         table = [kept([P, T], U32, "table%d" % a) for a in range(PASSES)]
         table_scales = kept([P, T], U8, "table_scales")
-        weight_scales_raw = kept([P, PASSES * H], U8, "weight_scales_raw")
-        weight_scales = kept([P, PASSES * H], U8, "weight_scales")
+        weight_scales_raw = kept([P, H], U8, "weight_scales_raw")
+        w2_rows = kept([P, H // 4], I32, "w2_rows")
+        w2_plane1 = kept([P, H], U8, "w2_plane1")
         table_rows = kept([P, T // 4], I32, "table_rows")
-        w2_rows = kept([P, PASSES * H // 4], I32, "w2_rows")
         carrier_plane1 = kept([P, S], U8, "carrier_plane1")
         w2_raw = keep.tile([P, PASSES * 2 * H], U8, name="w2_raw", tag="packed_raw", align_bytes=64)
         w2_codes = kept([P, PASSES * 2 * H], U8, "w2_codes")
         amp_sb = kept([P, GROUPS, PACK], F32, "amp_sb")
-        w4_rows = kept([P, N // 4], I32, "w4_rows")
         gain_sb = kept([P, PACK], F32, "gain_sb")
         one = kept([P, 1], F32, "one")
         quarter_pi = kept([P, 1], F32, "quarter_pi")
@@ -69,6 +68,7 @@ def tile_list_anycast_steering_features_kernel(
         nc.gpsimd.memset(weight_scales_raw[:].bitcast(I32), 0)
         nc.vector.memset(table_scales[:].bitcast(I32), 0)
         nc.gpsimd.memset(carrier_plane1[:].bitcast(I32), 0)
+        nc.gpsimd.memset(w2_plane1[:].bitcast(I32), 0)
         nc.vector.memset(one[:], 1.0)
         nc.vector.tensor_scalar(out=quarter_pi[:], in0=one[:], scalar1=math.pi / 4, scalar2=None, op0=ALU.mult)
 
@@ -95,17 +95,16 @@ def tile_list_anycast_steering_features_kernel(
             )
         nc.sync.dma_start(lists[1][:], offs2)
         nc.sync.dma_start(lists[0][:], offs)
+        nc.sync.dma_start(lists[2][:], offs3)
         nc.sync.dma_start(
             out=w2_raw[:].bitcast(I32).rearrange("p (a c) -> p a c", a=PASSES),
             in_=w2_words.bitcast(I32).rearrange("a p c -> p a c"),
         )
-        load_table(0)
-        nc.sync.dma_start(lists[2][:], offs3)
         for q in range(QUADS):
             nc.sync.dma_start(
-                out=w2_rows[32 * q : 32 * q + 4, :].rearrange("r (a c) -> r a c", a=PASSES),
-                in_=w2_scales[:, 4 * q : 4 * q + 4, :].bitcast(I32).rearrange("a r c -> r a c"),
+                out=w2_rows[32 * q : 32 * q + 8, :], in_=w2_scales[:, 4 * q : 4 * q + 4, :].bitcast(I32)
             )
+        load_table(0)
         load_weight("w1", w1, 0, 0, 1)
         load_weight("w1", w1, 0, 1, 1)
         load_table(1)
@@ -113,27 +112,10 @@ def tile_list_anycast_steering_features_kernel(
         nc.sync.dma_start(out=amp_sb[:], in_=amp.rearrange("(b p t) -> p b t", p=P, t=PACK))
         nc.sync.dma_start(out=gain_sb[:], in_=gain.rearrange("(p t) -> p t", t=PACK))
         load_weight("w1", w1, 1, 1, 1)
-        for q in range(QUADS):
-            nc.sync.dma_start(
-                out=w4_rows[32 * q : 32 * q + 8, :], in_=w4_scales[:, 4 * q : 4 * q + 4, :].bitcast(I32)
-            )
-
 
         for q in range(QUADS):
             rows = slice(32 * q, 32 * q + 8)
             nc.vector.tensor_copy(out=table_scales[rows, :].bitcast(I32), in_=table_rows[rows, :])
-        nc.scalar.copy(
-            out=w2_codes[:].bitcast(U16).rearrange("p (g t m) -> p g t m", t=PACK, m=P),
-            in_=w2_raw[:].bitcast(U16).rearrange("p (g m t) -> p g t m", t=PACK, m=P),
-        )
-        for q in range(QUADS):
-            rows = slice(32 * q, 32 * q + 4)
-            nc.scalar.copy(out=weight_scales_raw[rows, :].bitcast(U32), in_=w2_rows[rows, :].bitcast(U32))
-        w4_raw = keep.tile([P, GROUPS * N], I32, name="w4_raw", tag="packed_raw", align_bytes=64)
-        nc.sync.dma_start(
-            out=w4_raw[:].rearrange("p (a c) -> p a c", a=GROUPS),
-            in_=w4_words.rearrange("a p c i -> p a (c i)").bitcast(I32),
-        )
 
         picked = {}
         picked_scales = {}
@@ -151,8 +133,9 @@ def tile_list_anycast_steering_features_kernel(
         codes = {}
         planes = {}
 
-        def round_weight(name, b, a, engines):
-            tile = kept([P, GROUP * PACK], BF16, "grouped_%s_%d_%d" % (name, b, a))
+        def round_weight(name, b, a, engines, tag=None):
+            label = "grouped_%s_%d_%d" % (name, b, a)
+            tile = keep.tile([P, GROUP * PACK], BF16, name=label, tag=tag or label, align_bytes=64)
             grouped[name, b, a] = tile
             dst = tile[:].rearrange("p (t m j) -> p m j t", t=PACK, j=PACK)
             pieces = raw[name, b, a]
@@ -195,7 +178,7 @@ def tile_list_anycast_steering_features_kernel(
                     nc.tensor.matmul_mx(
                         out=banks[t][:],
                         lhsT=w2_codes[:, 2 * c0 : 2 * (c0 + P)].bitcast(FP4X4),
-                        lhsT_scale=weight_scales[:, c0 : c0 + P],
+                        lhsT_scale=(weight_scales if a == 0 else w2_plane1)[:, c0 - a * H : c0 - a * H + P],
                         rhs=picked[1, a][:].bitcast(FP8X4),
                         rhs_scale=(picked_scales[1] if a == 0 else carrier_plane1)[:],
                         start=(a == 0),
@@ -264,63 +247,80 @@ def tile_list_anycast_steering_features_kernel(
         nc.gpsimd.dma_start(
             out=carrier_plane1[0 : P - 4, :].bitcast(I32), in_=picked_scales[1][4:P, :].bitcast(I32)
         )
+        for q in range(QUADS):
+            rows = slice(32 * q, 32 * q + 8)
+            nc.scalar.copy(out=weight_scales_raw[rows, :].bitcast(U32), in_=w2_rows[rows, :].bitcast(U32))
+        nc.scalar.copy(
+            out=w2_codes[:].bitcast(U16).rearrange("p (g t m) -> p g t m", t=PACK, m=P),
+            in_=w2_raw[:].bitcast(U16).rearrange("p (g m t) -> p g t m", t=PACK, m=P),
+        )
+        w4_raw = keep.tile([P, GROUPS * N], I32, name="w4_raw", tag="packed_raw", align_bytes=64)
+        nc.sync.dma_start(
+            out=w4_raw[:].rearrange("p (a c) -> p a c", a=GROUPS),
+            in_=w4_words.rearrange("a p c i -> p a (c i)").bitcast(I32),
+        )
         gather_scales(0)
         gather_scales(2)
-        gather_words(0, 0)
-        gather_words(1, 0)
-        round_weight("w1", 0, 0, ["scalar"])
-        load_weight("w3", w3, 0, 0, 1)
-        gather_words(2, 0)
+        weight_scales = keep.tile([P, H], U8, name="weight_scales", tag="table_rows", align_bytes=64)
         nc.vector.tensor_copy(
             out=weight_scales[:].rearrange("p (g t m) -> p g t m", t=PACK, m=P),
             in_=weight_scales_raw[:].rearrange("p (g m t) -> p g t m", t=PACK, m=P),
         )
+        nc.gpsimd.dma_start(out=w2_plane1[0 : P - 4, :].bitcast(I32), in_=weight_scales[4:P, :].bitcast(I32))
         w4_scales_raw = keep.tile([P, N], U8, name="w4_scales_raw", tag="weight_scales_raw", align_bytes=64)
         nc.gpsimd.memset(w4_scales_raw[:].bitcast(I32), 0)
         for q in range(QUADS):
-            rows = slice(32 * q, 32 * q + 8)
-            nc.gpsimd.tensor_copy(out=w4_scales_raw[rows, :].bitcast(I32), in_=w4_rows[rows, :])
+            nc.gpsimd.dma_start(
+                out=w4_scales_raw[32 * q : 32 * q + 8, :].bitcast(I32),
+                in_=w4_scales[:, 4 * q : 4 * q + 4, :].bitcast(I32),
+            )
+        round_weight("w1", 0, 0, ["scalar"])
+        load_weight("w3", w3, 0, 0, 1)
+        gather_words(0, 0)
         quantize_weight("w1", 0, 0)
+        gather_words(1, 0)
+        gather_words(2, 0)
         round_weight("w1", 0, 1, ["scalar"])
         load_weight("w3", w3, 0, 1, 1)
         gather_words(0, 1, "grouped_w1_0_0")
         quantize_weight("w1", 0, 1)
-        gather_words(1, 1, "grouped_w1_0_1")
         prefix0 = product("w1", 0, 0)
+        gather_words(1, 1, "grouped_w1_0_1")
         carrier0 = carrier_product(0)
         round_weight("w1", 1, 0, ["scalar"])
         load_weight("w3", w3, 1, 0, 1)
-        gather_words(2, 1, "codes_w1_0_1")
+        gather_words(2, 1, "codes_w1_0_0")
         quantize_weight("w1", 1, 0)
-        round_weight("w1", 1, 1, ["scalar"])
-        lifted_path(0, prefix0, carrier0)
+        round_weight("w1", 1, 1, ["vector"], "grouped_w1_1_0")
         quantize_weight("w1", 1, 1)
+        lifted_path(0, prefix0, carrier0)
         prefix1 = product("w1", 0, 1)
         carrier1 = carrier_product(1)
-        round_weight("w3", 0, 0, ["vector"])
+        round_weight("w3", 0, 0, ["vector"], "grouped_w1_1_0")
         load_weight("w3", w3, 1, 1, 2)
-        w4_codes = keep.tile([P, GROUPS * N], I32, name="w4_codes", tag="codes_w1_1_0", align_bytes=64)
-        nc.vector.tensor_copy(
-            out=w4_codes[:].bitcast(I32).rearrange("p (g t m) -> p g m t", t=PACK, m=P),
-            in_=w4_raw[:].bitcast(I32).rearrange("p (g m t) -> p g m t", t=PACK, m=P),
+        quantize_weight("w3", 0, 0)
+        round_weight("w3", 0, 1, ["vector"], "grouped_w1_1_0")
+        quantize_weight("w3", 0, 1)
+        lifted_path(1, prefix1, carrier1)
+        site0 = product("w3", 2, 0)
+        round_weight("w3", 1, 0, ["scalar"])
+        round_weight("w3", 1, 1, ["vector", "scalar"])
+        w4_codes = keep.tile([P, GROUPS * N], U32, name="w4_codes", tag="codes_w1_1_0", align_bytes=64)
+        nc.scalar.copy(
+            out=w4_codes[:].bitcast(U32).rearrange("p (g t m) -> p g m t", t=PACK, m=P),
+            in_=w4_raw[:].bitcast(U32).rearrange("p (g m t) -> p g m t", t=PACK, m=P),
         )
         w4_planes = keep.tile([P, N], U8, name="w4_planes", tag="plane_w1_1_0", align_bytes=64)
         nc.vector.tensor_copy(
             out=w4_planes[:].rearrange("p (t m) -> p t m", t=PACK),
             in_=w4_scales_raw[:].rearrange("p (m t) -> p t m", t=PACK),
         )
-        quantize_weight("w3", 0, 0)
-        round_weight("w3", 0, 1, ["vector"])
-        lifted_path(1, prefix1, carrier1)
-        quantize_weight("w3", 0, 1)
-        site0 = product("w3", 2, 0)
-        round_weight("w3", 1, 0, ["scalar"])
-        round_weight("w3", 1, 1, ["vector", "scalar"])
-        woven0 = make_h(0, 0, site0, "scalar", S)
         quantize_weight("w3", 1, 0)
         quantize_weight("w3", 1, 1)
         site1 = product("w3", 2, 1)
-        quantize_h(0, 0, woven0, S)
+        woven0 = [make_h(0, u, site0, ["scalar", "scalar"][u]) for u in range(2)]
+        quantize_h(0, 0, woven0[0])
+        quantize_h(0, 1, woven0[1])
         y_banks = [[psum.tile([P, S], F32, name="bank", tag="bank") for pair in range(2)] for u in range(2)]
         for u in range(2):
             last_product(0, u, y_banks)
@@ -338,7 +338,7 @@ def tile_list_anycast_steering_features_kernel(
             y = kept([P, PACK, HALF], F32, "y%d" % u)
             for t in range(PACK):
                 sums = y_banks[u][t // 2][:, (t % 2) * HALF : (t % 2 + 1) * HALF]
-                if t // 2 == 0:
+                if u == 1 or t < 2:
                     nc.scalar.activation(out=y[:, t, :], in_=sums, func=ACT.Copy, scale=gain_sb[:, t : t + 1])
                 else:
                     nc.vector.tensor_scalar(

@@ -125,8 +125,9 @@ def tile_list_anycast_steering_features_kernel(
             picked[i, a] = keep.tile([P, S], U32, name=name, tag=tag or name, align_bytes=64)
             nc.vector.tensor_copy(out=picked[i, a][:], in_=table[a][:].indirect(lists[i][:]))
 
-        def gather_scales(i):
-            picked_scales[i] = kept([P, S], U8, "picked_scales%d" % i)
+        def gather_scales(i, tag=None):
+            name = "picked_scales%d" % i
+            picked_scales[i] = keep.tile([P, S], U8, name=name, tag=tag or name, align_bytes=64)
             nc.vector.tensor_copy(out=picked_scales[i][:], in_=table_scales[:].indirect(lists[i][:]))
 
         grouped = {}
@@ -145,7 +146,10 @@ def tile_list_anycast_steering_features_kernel(
                 m0 = u * share
                 src = pieces[m0 // per_piece][:].rearrange("p j (m t) -> p m j t", t=PACK)
                 l0 = m0 % per_piece
-                copy_on(engine, dst[:, m0 : m0 + share], src[:, l0 : l0 + share])
+                steps = 2 if engine == "vector" else 1
+                for k in range(steps):
+                    ts = slice(k * PACK // steps, (k + 1) * PACK // steps)
+                    copy_on(engine, dst[:, m0 : m0 + share, :, ts], src[:, l0 : l0 + share, :, ts])
 
         def quantize_weight(name, b, a):
             codes[name, b, a] = kept([P, GROUP], U32, "codes_%s_%d_%d" % (name, b, a))
@@ -222,6 +226,20 @@ def tile_list_anycast_steering_features_kernel(
             interleave(engine, woven[:], rows[:])
             return woven
 
+        def make_h_wide(b, site, engines):
+            rows = kept([P, PACK, S], BF16, "h_rows%d" % b)
+            for t in range(PACK):
+                nc.vector.scalar_tensor_tensor(
+                    out=rows[:, t, :], in0=lifted[b, t][:], scalar=amp_sb[:, b, t : t + 1], in1=site[t][:],
+                    op0=ALU.subtract, op1=ALU.max,
+                )
+            woven = []
+            for u in range(2):
+                half = kept([P, PACK * HALF], BF16, "h_woven%d_%d" % (b, u))
+                interleave(engines[u], half[:], rows[:, :, u * HALF : (u + 1) * HALF])
+                woven.append(half)
+            return woven
+
         def quantize_h(b, u, woven, width=HALF):
             words = kept([P, width], U32, "h_codes%d_%d" % (b, u))
             plane = kept([P, width], U8, "h_plane%d_%d" % (b, u))
@@ -289,7 +307,7 @@ def tile_list_anycast_steering_features_kernel(
         carrier0 = carrier_product(0)
         round_weight("w1", 1, 0, ["scalar"])
         load_weight("w3", w3, 1, 0, 1)
-        gather_words(2, 1, "codes_w1_0_0")
+        gather_words(2, 1, "codes_w1_0_1")
         quantize_weight("w1", 1, 0)
         round_weight("w1", 1, 1, ["vector"], "grouped_w1_1_0")
         quantize_weight("w1", 1, 1)
@@ -297,14 +315,14 @@ def tile_list_anycast_steering_features_kernel(
         prefix1 = product("w1", 0, 1)
         carrier1 = carrier_product(1)
         round_weight("w3", 0, 0, ["vector"], "grouped_w1_1_0")
-        load_weight("w3", w3, 1, 1, 2)
+        load_weight("w3", w3, 1, 1, 1)
         quantize_weight("w3", 0, 0)
         round_weight("w3", 0, 1, ["vector"], "grouped_w1_1_0")
         quantize_weight("w3", 0, 1)
         lifted_path(1, prefix1, carrier1)
         site0 = product("w3", 2, 0)
         round_weight("w3", 1, 0, ["scalar"])
-        round_weight("w3", 1, 1, ["vector", "scalar"])
+        round_weight("w3", 1, 1, ["scalar"])
         w4_codes = keep.tile([P, GROUPS * N], U32, name="w4_codes", tag="codes_w1_1_0", align_bytes=64)
         nc.scalar.copy(
             out=w4_codes[:].bitcast(U32).rearrange("p (g t m) -> p g m t", t=PACK, m=P),
@@ -318,7 +336,7 @@ def tile_list_anycast_steering_features_kernel(
         quantize_weight("w3", 1, 0)
         quantize_weight("w3", 1, 1)
         site1 = product("w3", 2, 1)
-        woven0 = [make_h(0, u, site0, ["scalar", "scalar"][u]) for u in range(2)]
+        woven0 = make_h_wide(0, site0, ["scalar", "scalar"])
         quantize_h(0, 0, woven0[0])
         quantize_h(0, 1, woven0[1])
         y_banks = [[psum.tile([P, S], F32, name="bank", tag="bank") for pair in range(2)] for u in range(2)]
@@ -338,7 +356,7 @@ def tile_list_anycast_steering_features_kernel(
             y = kept([P, PACK, HALF], F32, "y%d" % u)
             for t in range(PACK):
                 sums = y_banks[u][t // 2][:, (t % 2) * HALF : (t % 2 + 1) * HALF]
-                if u == 1 or t < 2:
+                if True:
                     nc.scalar.activation(out=y[:, t, :], in_=sums, func=ACT.Copy, scale=gain_sb[:, t : t + 1])
                 else:
                     nc.vector.tensor_scalar(

@@ -72,6 +72,9 @@ def tile_list_anycast_steering_features_kernel(
         nc.vector.memset(one[:], 1.0)
         nc.vector.tensor_scalar(out=quarter_pi[:], in0=one[:], scalar1=math.pi / 4, scalar2=None, op0=ALU.mult)
 
+        warm = kept([P, 1], F32, "warm")
+        nc.scalar.activation(out=warm[:], in_=one[:], func=ACT.Sin, bias=quarter_pi[:], scale=0.5)
+
         raw = {}
 
         def load_weight(name, w, b, a, parts):

@@ -23,8 +23,12 @@ GROUP = P * PACK
 PASSES = K // GROUP
 GROUPS = H // GROUP
 QUADS = 4
-HALF = S // 2
+ROWS = 4
+HALVES = 2
+HALF = S // HALVES
 RAW_BUFS = 4
+SINE_BUFS = 4
+PSUM_BANKS = 8
 
 
 def tile_list_anycast_steering_features_kernel(
@@ -32,70 +36,67 @@ def tile_list_anycast_steering_features_kernel(
     w4_words, w4_scales, gain, out_0, out_1, out_2,
 ):
     nc = tc.nc
-
-    def copy_on(engine, out, in_):
-        if engine == "scalar":
-            nc.scalar.copy(out=out, in_=in_)
-        elif engine == "gpsimd":
-            nc.gpsimd.tensor_scalar(out=out, in0=in_, scalar1=1.0, scalar2=0.0, op0=ALU.mult, op1=ALU.add)
-        else:
-            nc.vector.tensor_copy(out=out, in_=in_)
+    vector_copy = nc.vector.tensor_copy
+    scalar_copy = nc.scalar.copy
 
     with ExitStack() as ctx:
         keep = ctx.enter_context(tc.tile_pool(name="keep", bufs=1))
-        stream = ctx.enter_context(tc.tile_pool(name="stream", bufs=1))
-        ring = ctx.enter_context(tc.tile_pool(name="ring", bufs=4))
-        psum = ctx.enter_context(tc.psum_pool(name="psum", bufs=8))
+        stream = ctx.enter_context(tc.tile_pool(name="stream", bufs=RAW_BUFS))
+        ring = ctx.enter_context(tc.tile_pool(name="ring", bufs=SINE_BUFS))
+        psum = ctx.enter_context(tc.psum_pool(name="psum", bufs=PSUM_BANKS))
 
-        def kept(shape, dtype, name):
-            return keep.tile(shape, dtype, name=name, align_bytes=64)
+        def kept(shape, dtype, name, after=None):
+            return keep.tile(shape, dtype, name=name, tag=after or name, align_bytes=64)
+
+        def quadrant_rows(q, passes):
+            return slice(32 * q, 32 * q + ROWS * passes)
+
+        def load_scale_rows(queue, tile, scales):
+            for q in range(QUADS):
+                queue.dma_start(
+                    out=tile[quadrant_rows(q, scales.shape[0]), :],
+                    in_=scales[:, ROWS * q : ROWS * (q + 1), :].bitcast(I32),
+                )
+
+        def lift_second_pass(plane, shared):
+            nc.gpsimd.dma_start(out=plane[0 : P - ROWS, :].bitcast(I32), in_=shared[ROWS:P, :].bitcast(I32))
 
         lists = [keep.tile([P, S // 16], U16, name="list%d" % i) for i in range(3)]
         table = [kept([P, T], U32, "table%d" % a) for a in range(PASSES)]
         table_scales = kept([P, T], U8, "table_scales")
-        weight_scales_raw = kept([P, H], U8, "weight_scales_raw")
+        w2_scales_raw = kept([P, H], U8, "w2_scales_raw")
         w2_rows = kept([P, H // 4], I32, "w2_rows")
         w2_plane1 = kept([P, H], U8, "w2_plane1")
         table_rows = kept([P, T // 4], I32, "table_rows")
         carrier_plane1 = kept([P, S], U8, "carrier_plane1")
-        w2_raw = keep.tile([P, PASSES * 2 * H], U8, name="w2_raw", tag="packed_raw", align_bytes=64)
+        w2_raw = kept([P, PASSES * 2 * H], U8, "w2_raw")
         w2_codes = kept([P, PASSES * 2 * H], U8, "w2_codes")
         amp_sb = kept([P, GROUPS, PACK], F32, "amp_sb")
         gain_sb = kept([P, PACK], F32, "gain_sb")
         one = kept([P, 1], F32, "one")
         quarter_pi = kept([P, 1], F32, "quarter_pi")
 
-        nc.gpsimd.memset(weight_scales_raw[:].bitcast(I32), 0)
+        nc.gpsimd.memset(w2_scales_raw[:].bitcast(I32), 0)
         nc.vector.memset(table_scales[:].bitcast(I32), 0)
         nc.gpsimd.memset(carrier_plane1[:].bitcast(I32), 0)
         nc.gpsimd.memset(w2_plane1[:].bitcast(I32), 0)
         nc.vector.memset(one[:], 1.0)
         nc.vector.tensor_scalar(out=quarter_pi[:], in0=one[:], scalar1=math.pi / 4, scalar2=None, op0=ALU.mult)
 
-        warm = kept([P, 1], F32, "warm")
-        nc.scalar.activation(out=warm[:], in_=one[:], func=ACT.Sin, bias=quarter_pi[:], scale=0.5)
-
+        weights = {"w1": w1, "w3": w3}
         raw = {}
 
-        def load_weight(name, w, b, a, parts):
-            rows = w[a * GROUP : (a + 1) * GROUP, :].rearrange("(p j) c -> p j c", j=PACK)
-            width = GROUP // parts
-            raw[name, b, a] = []
-            for u in range(parts):
-                piece = stream.tile([P, PACK, width], F32, name="piece", bufs=RAW_BUFS)
-                c0 = b * GROUP + u * width
-                nc.sync.dma_start(out=piece[:], in_=rows[:, :, c0 : c0 + width])
-                raw[name, b, a].append(piece)
+        def load_weight(name, b, a):
+            rows = weights[name][a * GROUP : (a + 1) * GROUP, :].rearrange("(p j) c -> p j c", j=PACK)
+            raw[name, b, a] = stream.tile([P, PACK, GROUP], F32, name="piece")
+            nc.sync.dma_start(out=raw[name, b, a][:], in_=rows[:, :, b * GROUP : (b + 1) * GROUP])
 
         def load_table(a):
             nc.sync.dma_start(
                 out=table[a][:].bitcast(I32), in_=tab_words[a].rearrange("p n i -> p (n i)").bitcast(I32)
             )
 
-        for q in range(QUADS):
-            nc.sync.dma_start(
-                out=table_rows[32 * q : 32 * q + 8, :], in_=tab_scales[:, 4 * q : 4 * q + 4, :].bitcast(I32)
-            )
+        load_scale_rows(nc.sync, table_rows, tab_scales)
         nc.sync.dma_start(lists[1][:], offs2)
         nc.sync.dma_start(lists[0][:], offs)
         nc.sync.dma_start(lists[2][:], offs3)
@@ -103,56 +104,41 @@ def tile_list_anycast_steering_features_kernel(
             out=w2_raw[:].bitcast(I32).rearrange("p (a c) -> p a c", a=PASSES),
             in_=w2_words.bitcast(I32).rearrange("a p c -> p a c"),
         )
-        for q in range(QUADS):
-            nc.sync.dma_start(
-                out=w2_rows[32 * q : 32 * q + 8, :], in_=w2_scales[:, 4 * q : 4 * q + 4, :].bitcast(I32)
-            )
+        load_scale_rows(nc.sync, w2_rows, w2_scales)
         load_table(0)
-        load_weight("w1", w1, 0, 0, 1)
-        load_weight("w1", w1, 0, 1, 1)
+        load_weight("w1", 0, 0)
+        load_weight("w1", 0, 1)
+        load_weight("w1", 1, 0)
         load_table(1)
-        load_weight("w1", w1, 1, 0, 1)
         nc.sync.dma_start(out=amp_sb[:], in_=amp.rearrange("(b p t) -> p b t", p=P, t=PACK))
         nc.sync.dma_start(out=gain_sb[:], in_=gain.rearrange("(p t) -> p t", t=PACK))
-        load_weight("w1", w1, 1, 1, 1)
+        load_weight("w1", 1, 1)
 
         for q in range(QUADS):
-            rows = slice(32 * q, 32 * q + 8)
-            nc.vector.tensor_copy(out=table_scales[rows, :].bitcast(I32), in_=table_rows[rows, :])
+            rows = quadrant_rows(q, PASSES)
+            vector_copy(out=table_scales[rows, :].bitcast(I32), in_=table_rows[rows, :])
 
         picked = {}
         picked_scales = {}
 
-        def gather_words(i, a, tag=None):
-            name = "picked%d_%d" % (i, a)
-            picked[i, a] = keep.tile([P, S], U32, name=name, tag=tag or name, align_bytes=64)
-            nc.vector.tensor_copy(out=picked[i, a][:], in_=table[a][:].indirect(lists[i][:]))
+        def gather_words(i, a, after=None):
+            picked[i, a] = kept([P, S], U32, "picked%d_%d" % (i, a), after)
+            vector_copy(out=picked[i, a][:], in_=table[a][:].indirect(lists[i][:]))
 
-        def gather_scales(i, tag=None):
-            name = "picked_scales%d" % i
-            picked_scales[i] = keep.tile([P, S], U8, name=name, tag=tag or name, align_bytes=64)
-            nc.vector.tensor_copy(out=picked_scales[i][:], in_=table_scales[:].indirect(lists[i][:]))
+        def gather_scales(i):
+            picked_scales[i] = kept([P, S], U8, "picked_scales%d" % i)
+            vector_copy(out=picked_scales[i][:], in_=table_scales[:].indirect(lists[i][:]))
 
         grouped = {}
         codes = {}
         planes = {}
 
-        def round_weight(name, b, a, engines, tag=None):
-            label = "grouped_%s_%d_%d" % (name, b, a)
-            tile = keep.tile([P, GROUP * PACK], BF16, name=label, tag=tag or label, align_bytes=64)
-            grouped[name, b, a] = tile
-            dst = tile[:].rearrange("p (t m j) -> p m j t", t=PACK, j=PACK)
-            pieces = raw[name, b, a]
-            share = P // len(engines)
-            per_piece = P // len(pieces)
-            for u, engine in enumerate(engines):
-                m0 = u * share
-                src = pieces[m0 // per_piece][:].rearrange("p j (m t) -> p m j t", t=PACK)
-                l0 = m0 % per_piece
-                steps = 2 if engine == "vector" else 1
-                for k in range(steps):
-                    ts = slice(k * PACK // steps, (k + 1) * PACK // steps)
-                    copy_on(engine, dst[:, m0 : m0 + share, :, ts], src[:, l0 : l0 + share, :, ts])
+        def round_weight(name, b, a, copy, after=None):
+            grouped[name, b, a] = kept([P, GROUP * PACK], BF16, "grouped_%s_%d_%d" % (name, b, a), after)
+            copy(
+                out=grouped[name, b, a][:].rearrange("p (t m j) -> p m j t", t=PACK, j=PACK),
+                in_=raw[name, b, a][:].rearrange("p j (m t) -> p m j t", t=PACK),
+            )
 
         def quantize_weight(name, b, a):
             codes[name, b, a] = kept([P, GROUP], U32, "codes_%s_%d_%d" % (name, b, a))
@@ -162,7 +148,7 @@ def tile_list_anycast_steering_features_kernel(
             )
 
         def product(name, i, b):
-            banks = [psum.tile([P, S], F32, name="bank", tag="bank") for t in range(PACK)]
+            banks = [psum.tile([P, S], F32, name="bank") for t in range(PACK)]
             for a in range(PASSES):
                 for t in range(PACK):
                     cols = slice(t * P, (t + 1) * P)
@@ -171,23 +157,23 @@ def tile_list_anycast_steering_features_kernel(
                         lhsT=codes[name, b, a][:, cols].bitcast(FP8X4),
                         lhsT_scale=planes[name, b, a][:, cols],
                         rhs=picked[i, a][:].bitcast(FP8X4),
-                        rhs_scale=picked_scales[i][4 * a : P, :],
+                        rhs_scale=picked_scales[i][ROWS * a : P, :],
                         start=(a == 0),
                         stop=(a == PASSES - 1),
                     )
             return banks
 
         def carrier_product(b):
-            banks = [psum.tile([P, S], F32, name="bank", tag="bank") for t in range(PACK)]
+            banks = [psum.tile([P, S], F32, name="bank") for t in range(PACK)]
             for a in range(PASSES):
                 for t in range(PACK):
-                    c0 = a * H + b * GROUP + t * P
+                    c0 = b * GROUP + t * P
                     nc.tensor.matmul_mx(
                         out=banks[t][:],
-                        lhsT=w2_codes[:, 2 * c0 : 2 * (c0 + P)].bitcast(FP4X4),
-                        lhsT_scale=(weight_scales if a == 0 else w2_plane1)[:, c0 - a * H : c0 - a * H + P],
+                        lhsT=w2_codes[:, 2 * (a * H + c0) : 2 * (a * H + c0 + P)].bitcast(FP4X4),
+                        lhsT_scale=(w2_plane0, w2_plane1)[a][:, c0 : c0 + P],
                         rhs=picked[1, a][:].bitcast(FP8X4),
-                        rhs_scale=(picked_scales[1] if a == 0 else carrier_plane1)[:],
+                        rhs_scale=(picked_scales[1], carrier_plane1)[a][:],
                         start=(a == 0),
                         stop=(a == PASSES - 1),
                     )
@@ -207,175 +193,154 @@ def tile_list_anycast_steering_features_kernel(
                     op0=ALU.mult, op1=ALU.add,
                 )
 
-        def interleave(engine, dst, src):
-            copy_on(
-                engine,
-                dst.rearrange("p (c i t) -> p c t i", i=PACK, t=PACK),
-                src.rearrange("p t (c i) -> p c t i", i=PACK),
-            )
-
-        h_codes = {}
-        h_planes = {}
-
-        def make_h(b, u, site, engine, width=HALF):
-            cols = slice(u * width, (u + 1) * width)
-            rows = kept([P, PACK, width], BF16, "h_rows%d_%d" % (b, u))
+        def h_rows(b, site, cols, name, after=None):
+            rows = kept([P, PACK, cols.stop - cols.start], BF16, name, after)
             for t in range(PACK):
                 nc.vector.scalar_tensor_tensor(
                     out=rows[:, t, :], in0=lifted[b, t][:, cols], scalar=amp_sb[:, b, t : t + 1], in1=site[t][:, cols],
                     op0=ALU.subtract, op1=ALU.max,
                 )
-            woven = kept([P, PACK * width], BF16, "h_woven%d_%d" % (b, u))
-            interleave(engine, woven[:], rows[:])
+            return rows
+
+        def weave(copy, rows, name):
+            woven = kept([P, PACK * HALF], BF16, name)
+            copy(
+                out=woven[:].rearrange("p (c i t) -> p c t i", i=PACK, t=PACK),
+                in_=rows.rearrange("p t (c i) -> p c t i", i=PACK),
+            )
             return woven
 
-        def make_h_wide(b, site, engines):
-            rows = kept([P, PACK, S], BF16, "h_rows%d" % b)
-            for t in range(PACK):
-                nc.vector.scalar_tensor_tensor(
-                    out=rows[:, t, :], in0=lifted[b, t][:], scalar=amp_sb[:, b, t : t + 1], in1=site[t][:],
-                    op0=ALU.subtract, op1=ALU.max,
-                )
-            woven = []
-            for u in range(2):
-                half = kept([P, PACK * HALF], BF16, "h_woven%d_%d" % (b, u))
-                interleave(engines[u], half[:], rows[:, :, u * HALF : (u + 1) * HALF])
-                woven.append(half)
-            return woven
+        h_codes = {}
+        h_planes = {}
 
-        def quantize_h(b, u, woven, width=HALF):
-            words = kept([P, width], U32, "h_codes%d_%d" % (b, u))
-            plane = kept([P, width], U8, "h_plane%d_%d" % (b, u))
-            nc.vector.quantize_mx(out=words[:].bitcast(FP8X4), scales=plane[:], in_=woven[:])
-            for v in range(width // HALF):
-                h_codes[b, u + v] = words[:, v * HALF : (v + 1) * HALF]
-                h_planes[b, u + v] = plane[:, v * HALF : (v + 1) * HALF]
+        def quantize_h(b, u, woven):
+            h_codes[b, u] = kept([P, HALF], U32, "h_codes%d_%d" % (b, u))
+            h_planes[b, u] = kept([P, HALF], U8, "h_plane%d_%d" % (b, u))
+            nc.vector.quantize_mx(out=h_codes[b, u][:].bitcast(FP8X4), scales=h_planes[b, u][:], in_=woven[:])
 
-        def last_product(b, u, banks):
+        def y_sums(u, t):
+            return y_banks[u][t // 2][:, (t % 2) * HALF : (t % 2 + 1) * HALF]
+
+        def last_pass(b, u):
             for t in range(PACK):
                 c0 = b * N + t * P
                 nc.tensor.matmul_mx(
-                    out=banks[u][t // 2][:, (t % 2) * HALF : (t % 2 + 1) * HALF],
+                    out=y_sums(u, t),
                     lhsT=w4_codes[:, c0 : c0 + P].bitcast(FP8X4),
-                    lhsT_scale=w4_planes[4 * b : P, t * P : (t + 1) * P],
-                    rhs=h_codes[b, u].bitcast(FP8X4),
-                    rhs_scale=h_planes[b, u],
+                    lhsT_scale=w4_planes[ROWS * b : P, t * P : (t + 1) * P],
+                    rhs=h_codes[b, u][:].bitcast(FP8X4),
+                    rhs_scale=h_planes[b, u][:],
                     start=(b == 0 and t % 2 == 0),
                     stop=(b == GROUPS - 1 and t % 2 == 1),
                 )
 
+        halves = [slice(u * HALF, (u + 1) * HALF) for u in range(HALVES)]
+
         gather_scales(1)
-        nc.gpsimd.dma_start(
-            out=carrier_plane1[0 : P - 4, :].bitcast(I32), in_=picked_scales[1][4:P, :].bitcast(I32)
-        )
+        lift_second_pass(carrier_plane1, picked_scales[1])
         for q in range(QUADS):
-            rows = slice(32 * q, 32 * q + 8)
-            nc.scalar.copy(out=weight_scales_raw[rows, :].bitcast(U32), in_=w2_rows[rows, :].bitcast(U32))
-        nc.scalar.copy(
+            rows = quadrant_rows(q, PASSES)
+            scalar_copy(out=w2_scales_raw[rows, :].bitcast(U32), in_=w2_rows[rows, :].bitcast(U32))
+        scalar_copy(
             out=w2_codes[:].bitcast(U16).rearrange("p (g t m) -> p g t m", t=PACK, m=P),
             in_=w2_raw[:].bitcast(U16).rearrange("p (g m t) -> p g t m", t=PACK, m=P),
         )
-        w4_raw = keep.tile([P, GROUPS * N], I32, name="w4_raw", tag="packed_raw", align_bytes=64)
+        w4_raw = kept([P, GROUPS * N], I32, "w4_raw", after="w2_raw")
         nc.sync.dma_start(
             out=w4_raw[:].rearrange("p (a c) -> p a c", a=GROUPS),
             in_=w4_words.rearrange("a p c i -> p a (c i)").bitcast(I32),
         )
         gather_scales(0)
         gather_scales(2)
-        weight_scales = keep.tile([P, H], U8, name="weight_scales", tag="table_rows", align_bytes=64)
-        nc.vector.tensor_copy(
-            out=weight_scales[:].rearrange("p (g t m) -> p g t m", t=PACK, m=P),
-            in_=weight_scales_raw[:].rearrange("p (g m t) -> p g t m", t=PACK, m=P),
+        w2_plane0 = kept([P, H], U8, "w2_plane0", after="table_rows")
+        vector_copy(
+            out=w2_plane0[:].rearrange("p (g t m) -> p g t m", t=PACK, m=P),
+            in_=w2_scales_raw[:].rearrange("p (g m t) -> p g t m", t=PACK, m=P),
         )
-        nc.gpsimd.dma_start(out=w2_plane1[0 : P - 4, :].bitcast(I32), in_=weight_scales[4:P, :].bitcast(I32))
-        w4_scales_raw = keep.tile([P, N], U8, name="w4_scales_raw", tag="weight_scales_raw", align_bytes=64)
+        lift_second_pass(w2_plane1, w2_plane0)
+        w4_scales_raw = kept([P, N], U8, "w4_scales_raw", after="w2_scales_raw")
         nc.gpsimd.memset(w4_scales_raw[:].bitcast(I32), 0)
-        for q in range(QUADS):
-            nc.gpsimd.dma_start(
-                out=w4_scales_raw[32 * q : 32 * q + 8, :].bitcast(I32),
-                in_=w4_scales[:, 4 * q : 4 * q + 4, :].bitcast(I32),
-            )
-        round_weight("w1", 0, 0, ["scalar"])
-        load_weight("w3", w3, 0, 0, 1)
+        load_scale_rows(nc.gpsimd, w4_scales_raw[:].bitcast(I32), w4_scales)
+
+        round_weight("w1", 0, 0, scalar_copy)
+        load_weight("w3", 0, 0)
         gather_words(0, 0)
         quantize_weight("w1", 0, 0)
         gather_words(1, 0)
         gather_words(2, 0)
-        round_weight("w1", 0, 1, ["scalar"])
-        load_weight("w3", w3, 0, 1, 1)
-        gather_words(0, 1, "grouped_w1_0_0")
+        round_weight("w1", 0, 1, scalar_copy)
+        load_weight("w3", 0, 1)
+        gather_words(0, 1, after="grouped_w1_0_0")
         quantize_weight("w1", 0, 1)
         prefix0 = product("w1", 0, 0)
-        gather_words(1, 1, "grouped_w1_0_1")
+        gather_words(1, 1, after="grouped_w1_0_1")
         carrier0 = carrier_product(0)
-        round_weight("w1", 1, 0, ["scalar"])
-        load_weight("w3", w3, 1, 0, 1)
-        gather_words(2, 1, "codes_w1_0_1")
+        round_weight("w1", 1, 0, scalar_copy)
+        load_weight("w3", 1, 0)
+        gather_words(2, 1, after="codes_w1_0_1")
         quantize_weight("w1", 1, 0)
-        round_weight("w1", 1, 1, ["vector"], "grouped_w1_1_0")
+        round_weight("w1", 1, 1, scalar_copy)
         quantize_weight("w1", 1, 1)
+
         lifted_path(0, prefix0, carrier0)
         prefix1 = product("w1", 0, 1)
         carrier1 = carrier_product(1)
-        round_weight("w3", 0, 0, ["vector"], "grouped_w1_1_0")
-        load_weight("w3", w3, 1, 1, 1)
+        round_weight("w3", 0, 0, vector_copy, after="grouped_w1_1_1")
+        load_weight("w3", 1, 1)
         quantize_weight("w3", 0, 0)
-        round_weight("w3", 0, 1, ["vector"], "grouped_w1_1_0")
+        round_weight("w3", 0, 1, vector_copy, after="grouped_w1_1_1")
         quantize_weight("w3", 0, 1)
         lifted_path(1, prefix1, carrier1)
         site0 = product("w3", 2, 0)
-        round_weight("w3", 1, 0, ["scalar"])
-        round_weight("w3", 1, 1, ["scalar"])
-        w4_codes = keep.tile([P, GROUPS * N], U32, name="w4_codes", tag="codes_w1_1_0", align_bytes=64)
-        nc.scalar.copy(
-            out=w4_codes[:].bitcast(U32).rearrange("p (g t m) -> p g m t", t=PACK, m=P),
+        round_weight("w3", 1, 0, scalar_copy)
+        round_weight("w3", 1, 1, scalar_copy)
+        w4_codes = kept([P, GROUPS * N], U32, "w4_codes", after="codes_w1_1_0")
+        scalar_copy(
+            out=w4_codes[:].rearrange("p (g t m) -> p g m t", t=PACK, m=P),
             in_=w4_raw[:].bitcast(U32).rearrange("p (g m t) -> p g m t", t=PACK, m=P),
-        )
-        w4_planes = keep.tile([P, N], U8, name="w4_planes", tag="plane_w1_1_0", align_bytes=64)
-        nc.vector.tensor_copy(
-            out=w4_planes[:].rearrange("p (t m) -> p t m", t=PACK),
-            in_=w4_scales_raw[:].rearrange("p (m t) -> p t m", t=PACK),
         )
         quantize_weight("w3", 1, 0)
         quantize_weight("w3", 1, 1)
         site1 = product("w3", 2, 1)
-        woven0 = make_h_wide(0, site0, ["scalar", "scalar"])
-        quantize_h(0, 0, woven0[0])
-        quantize_h(0, 1, woven0[1])
-        y_banks = [[psum.tile([P, S], F32, name="bank", tag="bank") for pair in range(2)] for u in range(2)]
-        for u in range(2):
-            last_product(0, u, y_banks)
 
-        woven1 = [make_h(1, u, site1, ["scalar", "vector"][u]) for u in range(2)]
+        w4_planes = kept([P, N], U8, "w4_planes", after="grouped_w3_1_1")
+        vector_copy(
+            out=w4_planes[:].rearrange("p (t m) -> p t m", t=PACK),
+            in_=w4_scales_raw[:].rearrange("p (m t) -> p t m", t=PACK),
+        )
+        rows0 = h_rows(0, site0, slice(0, S), "h_rows0", after="grouped_w3_1_0")
+        woven0 = [weave(scalar_copy, rows0[:, :, halves[u]], "h_woven0_%d" % u) for u in range(HALVES)]
+        for u in range(HALVES):
+            quantize_h(0, u, woven0[u])
+        y_banks = [[psum.tile([P, S], F32, name="bank") for pair in range(PACK // 2)] for u in range(HALVES)]
+        for u in range(HALVES):
+            last_pass(0, u)
+
+        woven1 = []
+        for u, copy in enumerate((scalar_copy, vector_copy)):
+            rows1 = h_rows(1, site1, halves[u], "h_rows1_%d" % u)
+            woven1.append(weave(copy, rows1[:], "h_woven1_%d" % u))
+        for u in range(HALVES):
+            quantize_h(1, u, woven1[u])
+            last_pass(1, u)
+
         y_rows = out_0.rearrange("(p t) j -> p t j", t=PACK)
         y_words = out_1[0].rearrange("p m i -> p (m i)").bitcast(I32)
         y_plane = kept([P, S], U8, "y_plane")
         y_woven = []
-        for u in range(2):
-            quantize_h(1, u, woven1[u])
-            last_product(1, u, y_banks)
-        for u in range(2):
-            cols = slice(u * HALF, (u + 1) * HALF)
+        for u in range(HALVES):
             y = kept([P, PACK, HALF], F32, "y%d" % u)
             for t in range(PACK):
-                sums = y_banks[u][t // 2][:, (t % 2) * HALF : (t % 2 + 1) * HALF]
-                if True:
-                    nc.scalar.activation(out=y[:, t, :], in_=sums, func=ACT.Copy, scale=gain_sb[:, t : t + 1])
-                else:
-                    nc.vector.tensor_scalar(
-                        out=y[:, t, :], in0=sums, scalar1=gain_sb[:, t : t + 1], scalar2=None, op0=ALU.mult
-                    )
-            nc.sync.dma_start(out=y_rows[:, :, cols], in_=y[:])
-            woven = kept([P, PACK * HALF], BF16, "y_woven%d" % u)
-            interleave(["vector", "vector"][u], woven[:], y[:])
-            y_woven.append(woven)
-        for u in range(2):
-            cols = slice(u * HALF, (u + 1) * HALF)
+                nc.scalar.activation(out=y[:, t, :], in_=y_sums(u, t), func=ACT.Copy, scale=gain_sb[:, t : t + 1])
+            nc.sync.dma_start(out=y_rows[:, :, halves[u]], in_=y[:])
+            y_woven.append(weave(vector_copy, y[:], "y_woven%d" % u))
+        for u in range(HALVES):
             y_codes = kept([P, HALF], U32, "y_codes%d" % u)
-            nc.vector.quantize_mx(out=y_codes[:].bitcast(FP8X4), scales=y_plane[:, cols], in_=y_woven[u][:])
-            nc.sync.dma_start(out=y_words[:, cols], in_=y_codes[:].bitcast(I32))
+            nc.vector.quantize_mx(out=y_codes[:].bitcast(FP8X4), scales=y_plane[:, halves[u]], in_=y_woven[u][:])
+            nc.sync.dma_start(out=y_words[:, halves[u]], in_=y_codes[:].bitcast(I32))
         for q in range(QUADS):
-            queue = nc.sync if q % 2 == 0 else nc.scalar
+            queue = (nc.sync, nc.scalar)[q % 2]
             queue.dma_start(
-                out=out_2[0, 4 * q : 4 * q + 4, :].bitcast(I32), in_=y_plane[32 * q : 32 * q + 4, :].bitcast(I32)
+                out=out_2[0, ROWS * q : ROWS * (q + 1), :].bitcast(I32),
+                in_=y_plane[quadrant_rows(q, 1), :].bitcast(I32),
             )

import math
from contextlib import ExitStack

import concourse.mybir as mybir

K, T, S, H, N = 1024, 2048, 512, 1024, 512
FLOPS = 2 * (3 * K * H * S + H * N * S)

F32 = mybir.dt.float32
BF16 = mybir.dt.bfloat16
I32 = mybir.dt.int32
U32 = mybir.dt.uint32
U16 = mybir.dt.uint16
U8 = mybir.dt.uint8
FP8X4 = mybir.dt.float8_e4m3fn_x4
FP4X4 = mybir.dt.float4_e2m1fn_x4
ACT = mybir.ActivationFunctionType
ALU = mybir.AluOpType

P = 128
PACK = 4
GROUP = P * PACK
PASSES = K // GROUP
GROUPS = H // GROUP
QUADS = 4
ROWS = 4
HALVES = 2
HALF = S // HALVES
RAW_BUFS = 4
SINE_BUFS = 4
PSUM_BANKS = 8


def tile_list_anycast_steering_features_kernel(
    tc, tab_words, tab_scales, offs, offs2, offs3, w1, w2_words, w2_scales, w3, amp,
    w4_words, w4_scales, gain, out_0, out_1, out_2,
):
    nc = tc.nc
    vector_copy = nc.vector.tensor_copy
    scalar_copy = nc.scalar.copy

    with ExitStack() as ctx:
        keep = ctx.enter_context(tc.tile_pool(name="keep", bufs=1))
        stream = ctx.enter_context(tc.tile_pool(name="stream", bufs=RAW_BUFS))
        ring = ctx.enter_context(tc.tile_pool(name="ring", bufs=SINE_BUFS))
        psum = ctx.enter_context(tc.psum_pool(name="psum", bufs=PSUM_BANKS))

        def kept(shape, dtype, name, after=None):
            return keep.tile(shape, dtype, name=name, tag=after or name, align_bytes=64)

        def quadrant_rows(q, passes):
            return slice(32 * q, 32 * q + ROWS * passes)

        def load_scale_rows(queue, tile, scales):
            for q in range(QUADS):
                queue.dma_start(
                    out=tile[quadrant_rows(q, scales.shape[0]), :],
                    in_=scales[:, ROWS * q : ROWS * (q + 1), :].bitcast(I32),
                )

        def lift_second_pass(plane, shared):
            nc.gpsimd.dma_start(out=plane[0 : P - ROWS, :].bitcast(I32), in_=shared[ROWS:P, :].bitcast(I32))

        lists = [keep.tile([P, S // 16], U16, name="list%d" % i) for i in range(3)]
        table = [kept([P, T], U32, "table%d" % a) for a in range(PASSES)]
        table_scales = kept([P, T], U8, "table_scales")
        w2_scales_raw = kept([P, H], U8, "w2_scales_raw")
        w2_rows = kept([P, H // 4], I32, "w2_rows")
        w2_plane1 = kept([P, H], U8, "w2_plane1")
        table_rows = kept([P, T // 4], I32, "table_rows")
        carrier_plane1 = kept([P, S], U8, "carrier_plane1")
        w2_raw = kept([P, PASSES * 2 * H], U8, "w2_raw")
        w2_codes = kept([P, PASSES * 2 * H], U8, "w2_codes")
        amp_sb = kept([P, GROUPS, PACK], F32, "amp_sb")
        gain_sb = kept([P, PACK], F32, "gain_sb")
        one = kept([P, 1], F32, "one")
        quarter_pi = kept([P, 1], F32, "quarter_pi")

        nc.gpsimd.memset(w2_scales_raw[:].bitcast(I32), 0)
        nc.vector.memset(table_scales[:].bitcast(I32), 0)
        nc.gpsimd.memset(carrier_plane1[:].bitcast(I32), 0)
        nc.gpsimd.memset(w2_plane1[:].bitcast(I32), 0)
        nc.vector.memset(one[:], 1.0)
        nc.vector.tensor_scalar(out=quarter_pi[:], in0=one[:], scalar1=math.pi / 4, scalar2=None, op0=ALU.mult)

        weights = {"w1": w1, "w3": w3}
        raw = {}

        def load_weight(name, b, a):
            rows = weights[name][a * GROUP : (a + 1) * GROUP, :].rearrange("(p j) c -> p j c", j=PACK)
            raw[name, b, a] = stream.tile([P, PACK, GROUP], F32, name="piece")
            nc.sync.dma_start(out=raw[name, b, a][:], in_=rows[:, :, b * GROUP : (b + 1) * GROUP])

        def load_table(a):
            nc.sync.dma_start(
                out=table[a][:].bitcast(I32), in_=tab_words[a].rearrange("p n i -> p (n i)").bitcast(I32)
            )

        load_scale_rows(nc.sync, table_rows, tab_scales)
        nc.sync.dma_start(lists[1][:], offs2)
        nc.sync.dma_start(lists[0][:], offs)
        nc.sync.dma_start(lists[2][:], offs3)
        nc.sync.dma_start(
            out=w2_raw[:].bitcast(I32).rearrange("p (a c) -> p a c", a=PASSES),
            in_=w2_words.bitcast(I32).rearrange("a p c -> p a c"),
        )
        load_scale_rows(nc.sync, w2_rows, w2_scales)
        load_table(0)
        load_weight("w1", 0, 0)
        load_weight("w1", 0, 1)
        load_weight("w1", 1, 0)
        load_table(1)
        nc.sync.dma_start(out=amp_sb[:], in_=amp.rearrange("(b p t) -> p b t", p=P, t=PACK))
        nc.sync.dma_start(out=gain_sb[:], in_=gain.rearrange("(p t) -> p t", t=PACK))
        load_weight("w1", 1, 1)

        for q in range(QUADS):
            rows = quadrant_rows(q, PASSES)
            vector_copy(out=table_scales[rows, :].bitcast(I32), in_=table_rows[rows, :])

        picked = {}
        picked_scales = {}

        def gather_words(i, a, after=None):
            picked[i, a] = kept([P, S], U32, "picked%d_%d" % (i, a), after)
            vector_copy(out=picked[i, a][:], in_=table[a][:].indirect(lists[i][:]))

        def gather_scales(i):
            picked_scales[i] = kept([P, S], U8, "picked_scales%d" % i)
            vector_copy(out=picked_scales[i][:], in_=table_scales[:].indirect(lists[i][:]))

        grouped = {}
        codes = {}
        planes = {}

        def round_weight(name, b, a, copy, after=None):
            grouped[name, b, a] = kept([P, GROUP * PACK], BF16, "grouped_%s_%d_%d" % (name, b, a), after)
            copy(
                out=grouped[name, b, a][:].rearrange("p (t m j) -> p m j t", t=PACK, j=PACK),
                in_=raw[name, b, a][:].rearrange("p j (m t) -> p m j t", t=PACK),
            )

        def quantize_weight(name, b, a):
            codes[name, b, a] = kept([P, GROUP], U32, "codes_%s_%d_%d" % (name, b, a))
            planes[name, b, a] = kept([P, GROUP], U8, "plane_%s_%d_%d" % (name, b, a))
            nc.vector.quantize_mx(
                out=codes[name, b, a][:].bitcast(FP8X4), scales=planes[name, b, a][:], in_=grouped[name, b, a][:]
            )

        def product(name, i, b):
            banks = [psum.tile([P, S], F32, name="bank") for t in range(PACK)]
            for a in range(PASSES):
                for t in range(PACK):
                    cols = slice(t * P, (t + 1) * P)
                    nc.tensor.matmul_mx(
                        out=banks[t][:],
                        lhsT=codes[name, b, a][:, cols].bitcast(FP8X4),
                        lhsT_scale=planes[name, b, a][:, cols],
                        rhs=picked[i, a][:].bitcast(FP8X4),
                        rhs_scale=picked_scales[i][ROWS * a : P, :],
                        start=(a == 0),
                        stop=(a == PASSES - 1),
                    )
            return banks

        def carrier_product(b):
            banks = [psum.tile([P, S], F32, name="bank") for t in range(PACK)]
            for a in range(PASSES):
                for t in range(PACK):
                    c0 = b * GROUP + t * P
                    nc.tensor.matmul_mx(
                        out=banks[t][:],
                        lhsT=w2_codes[:, 2 * (a * H + c0) : 2 * (a * H + c0 + P)].bitcast(FP4X4),
                        lhsT_scale=(w2_plane0, w2_plane1)[a][:, c0 : c0 + P],
                        rhs=picked[1, a][:].bitcast(FP8X4),
                        rhs_scale=(picked_scales[1], carrier_plane1)[a][:],
                        start=(a == 0),
                        stop=(a == PASSES - 1),
                    )
            return banks

        lifted = {}

        def lifted_path(b, prefix, carrier):
            for t in range(PACK):
                sine = ring.tile([P, S], F32, name="sine")
                square = ring.tile([P, S], F32, name="square")
                nc.scalar.activation(out=sine[:], in_=prefix[t][:], func=ACT.Sin, bias=quarter_pi[:], scale=0.5)
                nc.scalar.activation(out=square[:], in_=sine[:], func=ACT.Square, scale=math.sqrt(2.0))
                lifted[b, t] = kept([P, S], F32, "lifted%d_%d" % (b, t))
                nc.vector.scalar_tensor_tensor(
                    out=lifted[b, t][:], in0=square[:], scalar=amp_sb[:, b, t : t + 1], in1=carrier[t][:],
                    op0=ALU.mult, op1=ALU.add,
                )

        def h_rows(b, site, cols, name, after=None):
            rows = kept([P, PACK, cols.stop - cols.start], BF16, name, after)
            for t in range(PACK):
                nc.vector.scalar_tensor_tensor(
                    out=rows[:, t, :], in0=lifted[b, t][:, cols], scalar=amp_sb[:, b, t : t + 1], in1=site[t][:, cols],
                    op0=ALU.subtract, op1=ALU.max,
                )
            return rows

        def weave(copy, rows, name):
            woven = kept([P, PACK * HALF], BF16, name)
            copy(
                out=woven[:].rearrange("p (c i t) -> p c t i", i=PACK, t=PACK),
                in_=rows.rearrange("p t (c i) -> p c t i", i=PACK),
            )
            return woven

        h_codes = {}
        h_planes = {}

        def quantize_h(b, u, woven):
            h_codes[b, u] = kept([P, HALF], U32, "h_codes%d_%d" % (b, u))
            h_planes[b, u] = kept([P, HALF], U8, "h_plane%d_%d" % (b, u))
            nc.vector.quantize_mx(out=h_codes[b, u][:].bitcast(FP8X4), scales=h_planes[b, u][:], in_=woven[:])

        def y_sums(u, t):
            return y_banks[u][t // 2][:, (t % 2) * HALF : (t % 2 + 1) * HALF]

        def last_pass(b, u):
            for t in range(PACK):
                c0 = b * N + t * P
                nc.tensor.matmul_mx(
                    out=y_sums(u, t),
                    lhsT=w4_codes[:, c0 : c0 + P].bitcast(FP8X4),
                    lhsT_scale=w4_planes[ROWS * b : P, t * P : (t + 1) * P],
                    rhs=h_codes[b, u][:].bitcast(FP8X4),
                    rhs_scale=h_planes[b, u][:],
                    start=(b == 0 and t % 2 == 0),
                    stop=(b == GROUPS - 1 and t % 2 == 1),
                )

        halves = [slice(u * HALF, (u + 1) * HALF) for u in range(HALVES)]

        gather_scales(1)
        lift_second_pass(carrier_plane1, picked_scales[1])
        for q in range(QUADS):
            rows = quadrant_rows(q, PASSES)
            scalar_copy(out=w2_scales_raw[rows, :].bitcast(U32), in_=w2_rows[rows, :].bitcast(U32))
        scalar_copy(
            out=w2_codes[:].bitcast(U16).rearrange("p (g t m) -> p g t m", t=PACK, m=P),
            in_=w2_raw[:].bitcast(U16).rearrange("p (g m t) -> p g t m", t=PACK, m=P),
        )
        w4_raw = kept([P, GROUPS * N], I32, "w4_raw", after="w2_raw")
        nc.sync.dma_start(
            out=w4_raw[:].rearrange("p (a c) -> p a c", a=GROUPS),
            in_=w4_words.rearrange("a p c i -> p a (c i)").bitcast(I32),
        )
        gather_scales(0)
        gather_scales(2)
        w2_plane0 = kept([P, H], U8, "w2_plane0", after="table_rows")
        vector_copy(
            out=w2_plane0[:].rearrange("p (g t m) -> p g t m", t=PACK, m=P),
            in_=w2_scales_raw[:].rearrange("p (g m t) -> p g t m", t=PACK, m=P),
        )
        lift_second_pass(w2_plane1, w2_plane0)
        w4_scales_raw = kept([P, N], U8, "w4_scales_raw", after="w2_scales_raw")
        nc.gpsimd.memset(w4_scales_raw[:].bitcast(I32), 0)
        load_scale_rows(nc.gpsimd, w4_scales_raw[:].bitcast(I32), w4_scales)

        round_weight("w1", 0, 0, scalar_copy)
        load_weight("w3", 0, 0)
        gather_words(0, 0)
        quantize_weight("w1", 0, 0)
        gather_words(1, 0)
        gather_words(2, 0)
        round_weight("w1", 0, 1, scalar_copy)
        load_weight("w3", 0, 1)
        gather_words(0, 1, after="grouped_w1_0_0")
        quantize_weight("w1", 0, 1)
        prefix0 = product("w1", 0, 0)
        gather_words(1, 1, after="grouped_w1_0_1")
        carrier0 = carrier_product(0)
        round_weight("w1", 1, 0, scalar_copy)
        load_weight("w3", 1, 0)
        gather_words(2, 1, after="codes_w1_0_1")
        quantize_weight("w1", 1, 0)
        round_weight("w1", 1, 1, scalar_copy)
        quantize_weight("w1", 1, 1)

        lifted_path(0, prefix0, carrier0)
        prefix1 = product("w1", 0, 1)
        carrier1 = carrier_product(1)
        round_weight("w3", 0, 0, vector_copy, after="grouped_w1_1_1")
        load_weight("w3", 1, 1)
        quantize_weight("w3", 0, 0)
        round_weight("w3", 0, 1, vector_copy, after="grouped_w1_1_1")
        quantize_weight("w3", 0, 1)
        lifted_path(1, prefix1, carrier1)
        site0 = product("w3", 2, 0)
        round_weight("w3", 1, 0, scalar_copy)
        round_weight("w3", 1, 1, scalar_copy)
        w4_codes = kept([P, GROUPS * N], U32, "w4_codes", after="codes_w1_1_0")
        scalar_copy(
            out=w4_codes[:].rearrange("p (g t m) -> p g m t", t=PACK, m=P),
            in_=w4_raw[:].bitcast(U32).rearrange("p (g m t) -> p g m t", t=PACK, m=P),
        )
        quantize_weight("w3", 1, 0)
        quantize_weight("w3", 1, 1)
        site1 = product("w3", 2, 1)

        w4_planes = kept([P, N], U8, "w4_planes", after="grouped_w3_1_1")
        vector_copy(
            out=w4_planes[:].rearrange("p (t m) -> p t m", t=PACK),
            in_=w4_scales_raw[:].rearrange("p (m t) -> p t m", t=PACK),
        )
        rows0 = h_rows(0, site0, slice(0, S), "h_rows0", after="grouped_w3_1_0")
        woven0 = [weave(scalar_copy, rows0[:, :, halves[u]], "h_woven0_%d" % u) for u in range(HALVES)]
        for u in range(HALVES):
            quantize_h(0, u, woven0[u])
        y_banks = [[psum.tile([P, S], F32, name="bank") for pair in range(PACK // 2)] for u in range(HALVES)]
        for u in range(HALVES):
            last_pass(0, u)

        woven1 = []
        for u, copy in enumerate((scalar_copy, vector_copy)):
            rows1 = h_rows(1, site1, halves[u], "h_rows1_%d" % u)
            woven1.append(weave(copy, rows1[:], "h_woven1_%d" % u))
        for u in range(HALVES):
            quantize_h(1, u, woven1[u])
            last_pass(1, u)

        y_rows = out_0.rearrange("(p t) j -> p t j", t=PACK)
        y_words = out_1[0].rearrange("p m i -> p (m i)").bitcast(I32)
        y_plane = kept([P, S], U8, "y_plane")
        y_woven = []
        for u in range(HALVES):
            y = kept([P, PACK, HALF], F32, "y%d" % u)
            for t in range(PACK):
                nc.scalar.activation(out=y[:, t, :], in_=y_sums(u, t), func=ACT.Copy, scale=gain_sb[:, t : t + 1])
            nc.sync.dma_start(out=y_rows[:, :, halves[u]], in_=y[:])
            y_woven.append(weave(vector_copy, y[:], "y_woven%d" % u))
        for u in range(HALVES):
            y_codes = kept([P, HALF], U32, "y_codes%d" % u)
            nc.vector.quantize_mx(out=y_codes[:].bitcast(FP8X4), scales=y_plane[:, halves[u]], in_=y_woven[u][:])
            nc.sync.dma_start(out=y_words[:, halves[u]], in_=y_codes[:].bitcast(I32))
        for q in range(QUADS):
            queue = (nc.sync, nc.scalar)[q % 2]
            queue.dma_start(
                out=out_2[0, ROWS * q : ROWS * (q + 1), :].bitcast(I32),
                in_=y_plane[quadrant_rows(q, 1), :].bitcast(I32),
            )
